import numpy as np
import ml_dtypes


def mxq(x, axis, fmt="e4m3"):
    dtype, down = {"e4m3": (ml_dtypes.float8_e4m3fn, 7), "e5m2": (ml_dtypes.float8_e5m2, 14)}[fmt]
    v = np.moveaxis(np.asarray(x, np.float32).astype(ml_dtypes.bfloat16).astype(np.float64), axis, -1)
    blocks = v.reshape(v.shape[:-1] + (-1, 32))
    amax = np.abs(blocks).max(-1, keepdims=True)
    byte = np.maximum(np.where(amax > 0, np.frexp(amax)[1] - 1 + 127, 0) - down, 1)
    scale = np.exp2(byte - 127.0)
    codes = (blocks / scale).astype(np.float32).astype(dtype).astype(np.float64)
    return np.moveaxis((codes * scale).reshape(v.shape), -1, axis)


WIDE = False


def mx_kscale(k):
    if not WIDE:
        return np.ones(k)
    levels = np.array([10, -10, 5, -5, 0])
    if k % 512:
        return np.exp2(np.random.permutation(np.resize(levels, k // 32))).repeat(32)
    a = np.empty((k // 512, 16))
    for p in range(k // 512):
        a[p, :8] = np.random.permutation(np.resize(levels, 8))
        for g in range(8):
            far = levels[np.abs(levels - a[p, g]) >= 10]
            a[p, g + 8] = far[np.random.randint(len(far))]
    return np.exp2(a.ravel()).repeat(32)


def f64(x):
    return np.asarray(x).astype(np.float64)


def striped8(idx):
    return np.asarray(idx).reshape(8, -1, 16).transpose(0, 2, 1).reshape(128, -1).astype(np.uint16)


def unstriped8(offs):
    return offs.reshape(8, 16, -1).transpose(0, 2, 1).reshape(8, -1).astype(np.int64)


def pick8(x, idx, run):
    r = np.arange(len(x))
    return x[r[:, None], idx[r % (8 * run) // run]]


E2M1 = np.array([0.0, 0.5, 1.0, 1.5, 2.0, 3.0, 4.0, 6.0, -0.0, -0.5, -1.0, -1.5, -2.0, -3.0, -4.0, -6.0])


def pack_weight(w, fmt):
    k, n = w.shape
    w = f64(np.asarray(w, np.float32).astype(ml_dtypes.bfloat16)).reshape(k // 32, 32, n)
    amax = np.abs(w).max(1)
    if fmt == "e4m3":
        byte = np.frexp(amax)[1] - 1 + 127 - 7
    else:
        mant, ex = np.frexp(amax / 6.0)
        byte = np.where(mant > 0.5, ex, ex - 1) + 127
    byte = np.clip(np.where(amax > 0, byte, 1), 1, 254)
    scaled = (w * np.exp2(127.0 - byte)[:, None, :]).reshape(k, n).astype(np.float32)
    by_word = np.ascontiguousarray(scaled.reshape(k // 512, 128, 4, n).transpose(0, 1, 3, 2))
    if fmt == "e4m3":
        words = by_word.astype(ml_dtypes.float8_e4m3fn).view(np.uint8)
    else:
        c = by_word.astype(ml_dtypes.float4_e2m1fn).view(np.uint8) & 0xF
        words = (c[..., 0::2] | (c[..., 1::2] << 4)).reshape(k // 512, 128, 2 * n)
    return np.ascontiguousarray(words), np.ascontiguousarray(byte.astype(np.uint8).reshape(k // 512, 16, n))


def unpack_weight(words, scales, fmt):
    g, _, n = scales.shape
    words = np.ascontiguousarray(words).reshape(g, 128, n, -1)
    if fmt == "e4m3":
        vals = words.view(ml_dtypes.float8_e4m3fn).astype(np.float64)
    else:
        nib = np.empty((g, 128, n, 4), np.uint8)
        nib[..., 0::2] = words & 0xF
        nib[..., 1::2] = words >> 4
        vals = E2M1[nib]
    vals = vals * np.repeat(np.exp2(scales.astype(np.float64) - 127.0), 8, axis=1)[..., None]
    return vals.transpose(0, 1, 3, 2).reshape(g * 512, n)


D, K, T, U, X, I, O, Q = 512, 512, 1024, 1024, 1024, 512, 2048, 128


def setup_inputs():
    n = np.random.standard_normal
    idx = np.stack([np.random.permutation(X)[:I] for _ in range(8)])
    idx2 = np.stack([np.random.permutation(O)[:I] for _ in range(8)])
    idx3 = np.stack([np.random.permutation(O)[:I] for _ in range(8)])
    idx4 = np.stack([np.random.permutation(X)[:I] for _ in range(8)])
    idx5 = np.stack([np.random.permutation(X)[:I] for _ in range(8)])
    fd = mx_kscale(D)
    fk = mx_kscale(K)
    wqp = pack_weight(n((D, K)) * 1.0 / np.sqrt(D) * fd[:, None] * fk, "e4m3")
    cachep = pack_weight(n((K, T)) * 1.0 / np.sqrt(K) / fk[:, None], "e4m3")
    draftp = pack_weight(n((K, U)) * 1.0 / np.sqrt(K) / fk[:, None], "e2m1")
    archp = pack_weight(n((D, X)) * 1.0 / np.sqrt(D) * fd[:, None], "e4m3")
    return {
        "states": (n((D, Q)) * 0.95 / fd[:, None]).astype(np.float32),
        "wq_words": wqp[0],
        "wq_scales": wqp[1],
        "cache_words": cachep[0],
        "cache_scales": cachep[1],
        "draft_words": draftp[0],
        "draft_scales": draftp[1],
        "arch_words": archp[0],
        "arch_scales": archp[1],
        "offs": striped8(idx),
        "offs2": striped8(idx2),
        "offs3": striped8(idx3),
        "offs4": striped8(idx4),
        "offs5": striped8(idx5),
    }


def reference(states, wq_words, wq_scales, cache_words, cache_scales, draft_words, draft_scales, arch_words, arch_scales, offs, offs2, offs3, offs4, offs5):
    idx = unstriped8(offs)
    idx2 = unstriped8(offs2)
    idx3 = unstriped8(offs3)
    idx4 = unstriped8(offs4)
    idx5 = unstriped8(offs5)
    wqu = unpack_weight(wq_words, wq_scales, "e4m3")
    cacheu = unpack_weight(cache_words, cache_scales, "e4m3")
    draftu = unpack_weight(draft_words, draft_scales, "e2m1")
    archu = unpack_weight(arch_words, arch_scales, "e4m3")
    statesq = mxq(f64(states), 0, "e4m3")
    qv = wqu.T @ statesq
    qvq = mxq(qv, 0, "e4m3")
    a = qvq.T @ cacheu
    b = qvq.T @ draftu
    c0 = statesq.T @ archu
    ab = np.concatenate([a, b], axis=1)
    f1 = np.zeros((Q, O))
    f1[np.arange(Q)[:, None], idx2[np.arange(Q) % 128 // 16]] = pick8(c0, idx, 16)
    r = ab - f1
    f2 = np.zeros((Q, X))
    f2[np.arange(Q)[:, None], idx4[np.arange(Q) % 128 // 16]] = pick8(r, idx3, 16)
    cc = c0 + f2
    y = np.maximum(pick8(cc, idx5, 16), pick8(r, idx3, 16))
    return y

@@ -1,0 +1,207 @@
+from contextlib import ExitStack
+
+import concourse.mybir as mybir
+
+F32 = mybir.dt.float32
+BF16 = mybir.dt.bfloat16
+I32 = mybir.dt.int32
+U32 = mybir.dt.uint32
+U16 = mybir.dt.uint16
+U8 = mybir.dt.uint8
+FP8X4 = mybir.dt.float8_e4m3fn_x4
+FP4X4 = mybir.dt.float4_e2m1fn_x4
+COPY = mybir.ActivationFunctionType.Copy
+ADD = mybir.AluOpType.add
+SUB = mybir.AluOpType.subtract
+MAX = mybir.AluOpType.max
+
+P = 128
+PACK = 4
+D, K, T, U, X, I, O, Q = 512, 512, 1024, 1024, 1024, 512, 2048, 128
+BANK = 512
+HALF = I // 2
+LIST_HALF = HALF // 16
+C0_PASS = 256
+R_POOL = 640
+CC_VECTOR = 704
+
+FLOPS = 2 * Q * (D * K + K * T + K * U + D * X)
+
+
+def tile_attend_jointthree_sidethree_kernel(
+    tc, states, wq_words, wq_scales, cache_words, cache_scales, draft_words, draft_scales,
+    arch_words, arch_scales, offs, offs2, offs3, offs4, offs5, out,
+):
+    nc = tc.nc
+    with ExitStack() as ctx:
+        sb = ctx.enter_context(tc.tile_pool(name="sb", bufs=1))
+        ps = ctx.enter_context(tc.psum_pool(name="ps", bufs=1))
+
+        def load_plane_direct(name, scales, width):
+            plane = sb.tile([P, width], U8, name=name, align_bytes=64)
+            rows = scales[0].bitcast(I32)
+            for g in range(4):
+                nc.sync.dma_start(out=plane[:].bitcast(I32)[32 * g : 32 * g + 4, :], in_=rows[4 * g : 4 * g + 4, :])
+            return plane
+
+        def load_plane(queue, plane, scales):
+            rows = scales[0].bitcast(I32).rearrange("(g h f) n -> g f h n", h=2, g=2)
+            words = plane[:].bitcast(I32).rearrange("p (h n) -> p h n", h=2)
+            for g in range(2):
+                queue.dma_start(out=words[64 * g : 64 * g + 4, :, :], in_=rows[g])
+
+        def spread_plane(plane, width):
+            words = plane[:].bitcast(I32)
+            n = width // 4
+            for g in range(2):
+                nc.vector.tensor_copy(out=words[64 * g + 32 : 64 * g + 36, 0:n], in_=words[64 * g : 64 * g + 4, n : 2 * n])
+
+        def load_list(name, source):
+            tile = sb.tile([P, I // 16], U16, name=name)
+            nc.sync.dma_start(tile[:], source)
+            return tile
+
+        arch_plane = sb.tile([P, 2 * X], U8, name="arch_plane", align_bytes=64)
+        wq_plane = sb.tile([P, 2 * K], U8, name="wq_plane", align_bytes=64)
+        nc.vector.memset(wq_plane[:].bitcast(I32), 0)
+
+        states_raw = sb.tile([P, PACK, Q], F32, name="states_raw")
+        nc.sync.dma_start(out=states_raw[:], in_=states.rearrange("(p t) q -> p t q", t=PACK))
+        load_plane(nc.scalar, arch_plane, arch_scales)
+        load_plane(nc.scalar, wq_plane, wq_scales)
+        arch_src = arch_words[0].rearrange("p n t -> p (n t)").bitcast(I32)
+        arch_w = []
+        for h in range(2):
+            tile = sb.tile([P, BANK], U32, name="arch_w%d" % h, align_bytes=64)
+            nc.sync.dma_start(out=tile[:].bitcast(I32), in_=arch_src[:, h * BANK : (h + 1) * BANK])
+            arch_w.append(tile)
+        wq_raw = sb.tile([P, K], U32, name="wq_raw", align_bytes=64)
+        nc.sync.dma_start(out=wq_raw[:].bitcast(I32), in_=wq_words[0].rearrange("p n t -> p (n t)").bitcast(I32))
+        list1 = load_list("list1", offs)
+        list2 = load_list("list2", offs2)
+        cache_w = sb.tile([P, T], U32, name="cache_w", align_bytes=64)
+        nc.sync.dma_start(out=cache_w[:].bitcast(I32), in_=cache_words[0].rearrange("p n t -> p (n t)").bitcast(I32))
+        cache_plane = load_plane_direct("cache_plane", cache_scales, T)
+        draft_w = sb.tile([P, 2 * U], U8, name="draft_w", align_bytes=64)
+        nc.sync.dma_start(out=draft_w[:].bitcast(I32), in_=draft_words[0].bitcast(I32))
+        draft_plane = load_plane_direct("draft_plane", draft_scales, U)
+        list3 = load_list("list3", offs3)
+        list4 = load_list("list4", offs4)
+        list5 = load_list("list5", offs5)
+
+        f1 = sb.tile([P, O], F32, name="f1")
+        nc.vector.memset(f1[:], 0.0)
+
+        states_bf = sb.tile([P, Q, PACK], BF16, name="states_bf", tag="states_then_deal", align_bytes=64)
+        nc.vector.tensor_copy(out=states_bf[:], in_=states_raw[:].rearrange("p t q -> p q t"))
+        spread_plane(arch_plane, X)
+        states_codes = sb.tile([P, Q], U32, name="states_codes", align_bytes=64)
+        states_plane = sb.tile([P, Q], U8, name="states_plane", align_bytes=64)
+        nc.vector.quantize_mx(
+            out=states_codes[:].bitcast(FP8X4), scales=states_plane[:],
+            in_=states_bf[:].rearrange("p q t -> p (q t)"),
+        )
+        spread_plane(wq_plane, K)
+        wq_dealt_plane = sb.tile([P, K], U8, name="wq_dealt_plane", tag="states_then_deal", align_bytes=64)
+        nc.vector.tensor_copy(
+            out=wq_dealt_plane[:].rearrange("p (t m) -> p m t", t=PACK),
+            in_=wq_plane[:, 0:K].rearrange("p (m t) -> p m t", t=PACK),
+        )
+        wq_dealt = sb.tile([P, K], U32, name="wq_dealt", align_bytes=64)
+        nc.vector.tensor_copy(
+            out=wq_dealt[:].bitcast(I32).rearrange("p (t m) -> p m t", t=PACK),
+            in_=wq_raw[:].bitcast(I32).rearrange("p (m t) -> p m t", t=PACK),
+        )
+
+        c0 = sb.tile([P, X], F32, name="c0")
+        c0_ps = []
+        for j in range(X // C0_PASS):
+            bank = ps.tile([P, C0_PASS], F32, name="c0_ps%d" % j)
+            lo = j * C0_PASS
+            nc.tensor.matmul_mx(
+                out=bank[:], lhsT=states_codes[:].bitcast(FP8X4), lhsT_scale=states_plane[:],
+                rhs=arch_w[lo // BANK][:, lo % BANK : lo % BANK + C0_PASS].bitcast(FP8X4),
+                rhs_scale=arch_plane[:, lo : lo + C0_PASS], start=True, stop=True,
+            )
+            nc.scalar.copy(out=c0[:, lo : lo + C0_PASS], in_=bank[:])
+            c0_ps.append(bank)
+
+        qv_ps = ps.tile([P, PACK, Q], F32, name="qv_ps", tag="last_bank")
+        for t in range(PACK):
+            nc.tensor.matmul_mx(
+                out=qv_ps[:, t, :], lhsT=wq_dealt[:, t * P : (t + 1) * P].bitcast(FP8X4),
+                lhsT_scale=wq_dealt_plane[:, t * P : (t + 1) * P],
+                rhs=states_codes[:].bitcast(FP8X4), rhs_scale=states_plane[:], start=True, stop=True,
+            )
+
+        def pick_and_place(h, tag):
+            picked = sb.tile([P, HALF], F32, name="c0_picked%d" % h, tag=tag, align_bytes=64)
+            cols = slice(h * LIST_HALF, (h + 1) * LIST_HALF)
+            nc.vector.tensor_copy(out=picked[:], in_=c0[:].indirect(list1[:, cols]))
+            nc.scalar.activation(f1[:].indirect(list2[:, cols]), picked[:], COPY)
+
+        qv_bf = sb.tile([P, Q, PACK], BF16, name="qv_bf", tag="qv_then_picked", align_bytes=64)
+        qv_view = qv_ps[:].rearrange("p t q -> p q t")
+        nc.scalar.copy(out=qv_bf[:, 0 : Q // 2, :], in_=qv_view[:, 0 : Q // 2, :])
+        pick_and_place(0, "picked_then_f2")
+        nc.vector.tensor_copy(out=qv_bf[:, Q // 2 : Q, :], in_=qv_view[:, Q // 2 : Q, :])
+        qv_codes = sb.tile([P, Q], U32, name="qv_codes", align_bytes=64)
+        qv_plane = sb.tile([P, Q], U8, name="qv_plane", align_bytes=64)
+        nc.vector.quantize_mx(
+            out=qv_codes[:].bitcast(FP8X4), scales=qv_plane[:],
+            in_=qv_bf[:].rearrange("p q t -> p (q t)"),
+        )
+        pick_and_place(1, "qv_then_picked")
+        f2 = sb.tile([P, X], F32, name="f2", tag="picked_then_f2", align_bytes=64)
+        nc.vector.memset(f2[:], 0.0)
+
+        ab_ps = []
+        for j in range(O // BANK):
+            bank = ps.tile([P, BANK], F32, name="ab_ps%d" % j, tag="last_bank" if j == O // BANK - 1 else "ab%d" % j)
+            lo = (j * BANK) % T
+            if j * BANK < T:
+                words = cache_w[:, lo : lo + BANK].bitcast(FP8X4)
+                plane = cache_plane[:, lo : lo + BANK]
+            else:
+                words = draft_w[:, 2 * lo : 2 * (lo + BANK)].bitcast(FP4X4)
+                plane = draft_plane[:, lo : lo + BANK]
+            nc.tensor.matmul_mx(
+                out=bank[:], lhsT=qv_codes[:].bitcast(FP8X4), lhsT_scale=qv_plane[:],
+                rhs=words, rhs_scale=plane, start=True, stop=True,
+            )
+            ab_ps.append(bank)
+
+        def pieces(lo, hi, width):
+            return [(max(lo, b), min(hi, b + width)) for b in range(lo // width * width, hi, width)]
+
+        ab_head = sb.tile([P, R_POOL], F32, name="ab_head")
+        for lo, hi in pieces(0, R_POOL, BANK):
+            nc.vector.tensor_copy(out=ab_head[:, lo:hi], in_=ab_ps[lo // BANK][:, lo % BANK : lo % BANK + hi - lo])
+
+        r = sb.tile([P, O], F32, name="r")
+        nc.gpsimd.tensor_tensor(out=r[:, 0:R_POOL], in0=ab_head[:], in1=f1[:, 0:R_POOL], op=SUB)
+        for lo, hi in pieces(R_POOL, O, BANK):
+            nc.vector.tensor_tensor(
+                out=r[:, lo:hi], in0=ab_ps[lo // BANK][:, lo % BANK : lo % BANK + hi - lo], in1=f1[:, lo:hi], op=SUB
+            )
+
+        r_picked = sb.tile([P, I], F32, name="r_picked")
+        nc.vector.tensor_copy(out=r_picked[:], in_=r[:].indirect(list3[:]))
+        nc.scalar.activation(f2[:].indirect(list4[:]), r_picked[:], COPY)
+
+        cc = sb.tile([P, X], F32, name="cc")
+        nc.gpsimd.tensor_tensor(out=cc[:, CC_VECTOR:X], in0=c0[:, CC_VECTOR:X], in1=f2[:, CC_VECTOR:X], op=ADD)
+        for lo, hi in pieces(0, CC_VECTOR, C0_PASS):
+            nc.vector.tensor_tensor(
+                out=cc[:, lo:hi], in0=c0_ps[lo // C0_PASS][:, lo % C0_PASS : lo % C0_PASS + hi - lo],
+                in1=f2[:, lo:hi], op=ADD,
+            )
+
+        cc_picked = [sb.tile([P, HALF], F32, name="cc_picked%d" % h) for h in range(2)]
+        nc.vector.tensor_copy(out=cc_picked[0][:], in_=cc[:].indirect(list5[:, 0:LIST_HALF]))
+        nc.scalar.activation(cc_picked[1][:], cc[:].indirect(list5[:, LIST_HALF : 2 * LIST_HALF]), COPY)
+        for h, queue in enumerate((nc.sync, nc.scalar)):
+            cols = slice(h * HALF, (h + 1) * HALF)
+            result = sb.tile([P, HALF], F32, name="result%d" % h)
+            nc.vector.tensor_tensor(out=result[:], in0=cc_picked[h][:], in1=r_picked[:, cols], op=MAX)
+            queue.dma_start(out=out[:, cols], in_=result[:])

@@ -116,7 +116,7 @@ def tile_attend_jointthree_sidethree_kernel(
         c0 = sb.tile([P, X], F32, name="c0")
         c0_ps = []
         for j in range(X // C0_PASS):
-            bank = ps.tile([P, C0_PASS], F32, name="c0_ps%d" % j)
+            bank = ps.tile([P, C0_PASS], F32, name="c0_ps%d" % j, tag="c0_bank%d" % j)
             lo = j * C0_PASS
             nc.tensor.matmul_mx(
                 out=bank[:], lhsT=states_codes[:].bitcast(FP8X4), lhsT_scale=states_plane[:],
@@ -126,7 +126,7 @@ def tile_attend_jointthree_sidethree_kernel(
             nc.scalar.copy(out=c0[:, lo : lo + C0_PASS], in_=bank[:])
             c0_ps.append(bank)
 
-        qv_ps = ps.tile([P, PACK, Q], F32, name="qv_ps", tag="last_bank")
+        qv_ps = ps.tile([P, PACK, Q], F32, name="qv_ps", tag="c0_bank3")
         for t in range(PACK):
             nc.tensor.matmul_mx(
                 out=qv_ps[:, t, :], lhsT=wq_dealt[:, t * P : (t + 1) * P].bitcast(FP8X4),
@@ -134,30 +134,27 @@ def tile_attend_jointthree_sidethree_kernel(
                 rhs=states_codes[:].bitcast(FP8X4), rhs_scale=states_plane[:], start=True, stop=True,
             )
 
-        def pick_and_place(h, tag):
-            picked = sb.tile([P, HALF], F32, name="c0_picked%d" % h, tag=tag, align_bytes=64)
+        for h in range(2):
+            picked = sb.tile([P, HALF], F32, name="c0_picked%d" % h)
             cols = slice(h * LIST_HALF, (h + 1) * LIST_HALF)
             nc.vector.tensor_copy(out=picked[:], in_=c0[:].indirect(list1[:, cols]))
             nc.scalar.activation(f1[:].indirect(list2[:, cols]), picked[:], COPY)
 
-        qv_bf = sb.tile([P, Q, PACK], BF16, name="qv_bf", tag="qv_then_picked", align_bytes=64)
-        qv_view = qv_ps[:].rearrange("p t q -> p q t")
-        nc.scalar.copy(out=qv_bf[:, 0 : Q // 2, :], in_=qv_view[:, 0 : Q // 2, :])
-        pick_and_place(0, "picked_then_f2")
-        nc.vector.tensor_copy(out=qv_bf[:, Q // 2 : Q, :], in_=qv_view[:, Q // 2 : Q, :])
+        qv_bf = sb.tile([P, Q, PACK], BF16, name="qv_bf", tag="qv_then_f2", align_bytes=64)
+        nc.vector.tensor_copy(out=qv_bf[:], in_=qv_ps[:].rearrange("p t q -> p q t"))
         qv_codes = sb.tile([P, Q], U32, name="qv_codes", align_bytes=64)
         qv_plane = sb.tile([P, Q], U8, name="qv_plane", align_bytes=64)
         nc.vector.quantize_mx(
             out=qv_codes[:].bitcast(FP8X4), scales=qv_plane[:],
             in_=qv_bf[:].rearrange("p q t -> p (q t)"),
         )
-        pick_and_place(1, "qv_then_picked")
-        f2 = sb.tile([P, X], F32, name="f2", tag="picked_then_f2", align_bytes=64)
+
+        f2 = sb.tile([P, X], F32, name="f2", tag="qv_then_f2", align_bytes=64)
         nc.vector.memset(f2[:], 0.0)
 
         ab_ps = []
         for j in range(O // BANK):
-            bank = ps.tile([P, BANK], F32, name="ab_ps%d" % j, tag="last_bank" if j == O // BANK - 1 else "ab%d" % j)
+            bank = ps.tile([P, BANK], F32, name="ab_ps%d" % j)
             lo = (j * BANK) % T
             if j * BANK < T:
                 words = cache_w[:, lo : lo + BANK].bitcast(FP8X4)

@@ -22,6 +22,7 @@ BANK = 512
 HALF = I // 2
 LIST_HALF = HALF // 16
 C0_PASS = 256
+C0_PASSES = ((0, 256), (256, 512), (512, 768), (768, 896), (896, 1024))
 R_POOL = 640
 CC_VECTOR = 704
 
@@ -61,14 +62,12 @@ def tile_attend_jointthree_sidethree_kernel(
             nc.sync.dma_start(tile[:], source)
             return tile
 
-        arch_plane = sb.tile([P, 2 * X], U8, name="arch_plane", align_bytes=64)
         wq_plane = sb.tile([P, 2 * K], U8, name="wq_plane", align_bytes=64)
         nc.vector.memset(wq_plane[:].bitcast(I32), 0)
 
         states_raw = sb.tile([P, PACK, Q], F32, name="states_raw")
         nc.sync.dma_start(out=states_raw[:], in_=states.rearrange("(p t) q -> p t q", t=PACK))
-        load_plane(nc.scalar, arch_plane, arch_scales)
-        load_plane(nc.scalar, wq_plane, wq_scales)
+        arch_plane = load_plane_direct("arch_plane", arch_scales, X)
         arch_src = arch_words[0].rearrange("p n t -> p (n t)").bitcast(I32)
         arch_w = []
         for h in range(2):
@@ -77,6 +76,7 @@ def tile_attend_jointthree_sidethree_kernel(
             arch_w.append(tile)
         wq_raw = sb.tile([P, K], U32, name="wq_raw", align_bytes=64)
         nc.sync.dma_start(out=wq_raw[:].bitcast(I32), in_=wq_words[0].rearrange("p n t -> p (n t)").bitcast(I32))
+        load_plane(nc.sync, wq_plane, wq_scales)
         list1 = load_list("list1", offs)
         list2 = load_list("list2", offs2)
         cache_w = sb.tile([P, T], U32, name="cache_w", align_bytes=64)
@@ -94,7 +94,6 @@ def tile_attend_jointthree_sidethree_kernel(
 
         states_bf = sb.tile([P, Q, PACK], BF16, name="states_bf", tag="states_then_deal", align_bytes=64)
         nc.vector.tensor_copy(out=states_bf[:], in_=states_raw[:].rearrange("p t q -> p q t"))
-        spread_plane(arch_plane, X)
         states_codes = sb.tile([P, Q], U32, name="states_codes", align_bytes=64)
         states_plane = sb.tile([P, Q], U8, name="states_plane", align_bytes=64)
         nc.vector.quantize_mx(
@@ -107,7 +106,7 @@ def tile_attend_jointthree_sidethree_kernel(
             out=wq_dealt_plane[:].rearrange("p (t m) -> p m t", t=PACK),
             in_=wq_plane[:, 0:K].rearrange("p (m t) -> p m t", t=PACK),
         )
-        wq_dealt = sb.tile([P, K], U32, name="wq_dealt", align_bytes=64)
+        wq_dealt = sb.tile([P, K], U32, name="wq_dealt", tag="wq_then_picked", align_bytes=64)
         nc.vector.tensor_copy(
             out=wq_dealt[:].bitcast(I32).rearrange("p (t m) -> p m t", t=PACK),
             in_=wq_raw[:].bitcast(I32).rearrange("p (m t) -> p m t", t=PACK),
@@ -115,18 +114,17 @@ def tile_attend_jointthree_sidethree_kernel(
 
         c0 = sb.tile([P, X], F32, name="c0")
         c0_ps = []
-        for j in range(X // C0_PASS):
-            bank = ps.tile([P, C0_PASS], F32, name="c0_ps%d" % j, tag="c0_bank%d" % j)
-            lo = j * C0_PASS
+        for j, (lo, hi) in enumerate(C0_PASSES):
+            bank = ps.tile([P, hi - lo], F32, name="c0_ps%d" % j, tag="bank%d" % j)
             nc.tensor.matmul_mx(
                 out=bank[:], lhsT=states_codes[:].bitcast(FP8X4), lhsT_scale=states_plane[:],
-                rhs=arch_w[lo // BANK][:, lo % BANK : lo % BANK + C0_PASS].bitcast(FP8X4),
-                rhs_scale=arch_plane[:, lo : lo + C0_PASS], start=True, stop=True,
+                rhs=arch_w[lo // BANK][:, lo % BANK : lo % BANK + hi - lo].bitcast(FP8X4),
+                rhs_scale=arch_plane[:, lo:hi], start=True, stop=True,
             )
-            nc.scalar.copy(out=c0[:, lo : lo + C0_PASS], in_=bank[:])
+            nc.scalar.copy(out=c0[:, lo:hi], in_=bank[:])
             c0_ps.append(bank)
 
-        qv_ps = ps.tile([P, PACK, Q], F32, name="qv_ps", tag="c0_bank3")
+        qv_ps = ps.tile([P, PACK, Q], F32, name="qv_ps", tag="bank4")
         for t in range(PACK):
             nc.tensor.matmul_mx(
                 out=qv_ps[:, t, :], lhsT=wq_dealt[:, t * P : (t + 1) * P].bitcast(FP8X4),
@@ -134,12 +132,13 @@ def tile_attend_jointthree_sidethree_kernel(
                 rhs=states_codes[:].bitcast(FP8X4), rhs_scale=states_plane[:], start=True, stop=True,
             )
 
-        for h in range(2):
-            picked = sb.tile([P, HALF], F32, name="c0_picked%d" % h)
+        def pick_and_place(h, tag):
+            picked = sb.tile([P, HALF], F32, name="c0_picked%d" % h, tag=tag, align_bytes=64)
             cols = slice(h * LIST_HALF, (h + 1) * LIST_HALF)
             nc.vector.tensor_copy(out=picked[:], in_=c0[:].indirect(list1[:, cols]))
             nc.scalar.activation(f1[:].indirect(list2[:, cols]), picked[:], COPY)
 
+        pick_and_place(0, "picked0")
         qv_bf = sb.tile([P, Q, PACK], BF16, name="qv_bf", tag="qv_then_f2", align_bytes=64)
         nc.vector.tensor_copy(out=qv_bf[:], in_=qv_ps[:].rearrange("p t q -> p q t"))
         qv_codes = sb.tile([P, Q], U32, name="qv_codes", align_bytes=64)
@@ -149,12 +148,13 @@ def tile_attend_jointthree_sidethree_kernel(
             in_=qv_bf[:].rearrange("p q t -> p (q t)"),
         )
 
+        pick_and_place(1, "wq_then_picked")
         f2 = sb.tile([P, X], F32, name="f2", tag="qv_then_f2", align_bytes=64)
         nc.vector.memset(f2[:], 0.0)
 
         ab_ps = []
         for j in range(O // BANK):
-            bank = ps.tile([P, BANK], F32, name="ab_ps%d" % j)
+            bank = ps.tile([P, BANK], F32, name="ab_ps%d" % j, tag="bank%d" % (5, 6, 7, 3)[j])
             lo = (j * BANK) % T
             if j * BANK < T:
                 words = cache_w[:, lo : lo + BANK].bitcast(FP8X4)

@@ -22,7 +22,7 @@ BANK = 512
 HALF = I // 2
 LIST_HALF = HALF // 16
 C0_PASS = 256
-C0_PASSES = ((0, 256), (256, 512), (512, 768), (768, 896), (896, 1024))
+C0_PASSES = ((0, 256), (256, 512), (512, 768), (768, 1024))
 R_POOL = 640
 CC_VECTOR = 704
 
@@ -93,20 +93,24 @@ def tile_attend_jointthree_sidethree_kernel(
         nc.vector.memset(f1[:], 0.0)
 
         states_bf = sb.tile([P, Q, PACK], BF16, name="states_bf", tag="states_then_deal", align_bytes=64)
-        nc.vector.tensor_copy(out=states_bf[:], in_=states_raw[:].rearrange("p t q -> p q t"))
+        for h in range(2):
+            cols = slice(h * Q // 2, (h + 1) * Q // 2)
+            nc.vector.tensor_copy(out=states_bf[:, cols, :], in_=states_raw[:, :, cols].rearrange("p t q -> p q t"))
         states_codes = sb.tile([P, Q], U32, name="states_codes", align_bytes=64)
         states_plane = sb.tile([P, Q], U8, name="states_plane", align_bytes=64)
-        nc.vector.quantize_mx(
-            out=states_codes[:].bitcast(FP8X4), scales=states_plane[:],
-            in_=states_bf[:].rearrange("p q t -> p (q t)"),
-        )
+        for h in range(2):
+            cols = slice(h * Q // 2, (h + 1) * Q // 2)
+            nc.vector.quantize_mx(
+                out=states_codes[:, cols].bitcast(FP8X4), scales=states_plane[:, cols],
+                in_=states_bf[:, cols, :].rearrange("p q t -> p (q t)"),
+            )
         spread_plane(wq_plane, K)
         wq_dealt_plane = sb.tile([P, K], U8, name="wq_dealt_plane", tag="states_then_deal", align_bytes=64)
         nc.vector.tensor_copy(
             out=wq_dealt_plane[:].rearrange("p (t m) -> p m t", t=PACK),
             in_=wq_plane[:, 0:K].rearrange("p (m t) -> p m t", t=PACK),
         )
-        wq_dealt = sb.tile([P, K], U32, name="wq_dealt", tag="wq_then_picked", align_bytes=64)
+        wq_dealt = sb.tile([P, K], U32, name="wq_dealt", align_bytes=64)
         nc.vector.tensor_copy(
             out=wq_dealt[:].bitcast(I32).rearrange("p (t m) -> p m t", t=PACK),
             in_=wq_raw[:].bitcast(I32).rearrange("p (m t) -> p m t", t=PACK),
@@ -124,7 +128,7 @@ def tile_attend_jointthree_sidethree_kernel(
             nc.scalar.copy(out=c0[:, lo:hi], in_=bank[:])
             c0_ps.append(bank)
 
-        qv_ps = ps.tile([P, PACK, Q], F32, name="qv_ps", tag="bank4")
+        qv_ps = ps.tile([P, PACK, Q], F32, name="qv_ps", tag="bank7")
         for t in range(PACK):
             nc.tensor.matmul_mx(
                 out=qv_ps[:, t, :], lhsT=wq_dealt[:, t * P : (t + 1) * P].bitcast(FP8X4),
@@ -135,7 +139,10 @@ def tile_attend_jointthree_sidethree_kernel(
         def pick_and_place(h, tag):
             picked = sb.tile([P, HALF], F32, name="c0_picked%d" % h, tag=tag, align_bytes=64)
             cols = slice(h * LIST_HALF, (h + 1) * LIST_HALF)
-            nc.vector.tensor_copy(out=picked[:], in_=c0[:].indirect(list1[:, cols]))
+            if h == 0:
+                nc.scalar.activation(picked[:], c0[:].indirect(list1[:, cols]), COPY)
+            else:
+                nc.vector.tensor_copy(out=picked[:], in_=c0[:].indirect(list1[:, cols]))
             nc.scalar.activation(f1[:].indirect(list2[:, cols]), picked[:], COPY)
 
         pick_and_place(0, "picked0")
@@ -148,13 +155,13 @@ def tile_attend_jointthree_sidethree_kernel(
             in_=qv_bf[:].rearrange("p q t -> p (q t)"),
         )
 
-        pick_and_place(1, "wq_then_picked")
+        pick_and_place(1, "picked1")
         f2 = sb.tile([P, X], F32, name="f2", tag="qv_then_f2", align_bytes=64)
         nc.vector.memset(f2[:], 0.0)
 
         ab_ps = []
         for j in range(O // BANK):
-            bank = ps.tile([P, BANK], F32, name="ab_ps%d" % j, tag="bank%d" % (5, 6, 7, 3)[j])
+            bank = ps.tile([P, BANK], F32, name="ab_ps%d" % j, tag="bank%d" % (4 + j))
             lo = (j * BANK) % T
             if j * BANK < T:
                 words = cache_w[:, lo : lo + BANK].bitcast(FP8X4)

from contextlib import ExitStack

import concourse.mybir as mybir

F32 = mybir.dt.float32
BF16 = mybir.dt.bfloat16
I32 = mybir.dt.int32
U32 = mybir.dt.uint32
U16 = mybir.dt.uint16
U8 = mybir.dt.uint8
FP8X4 = mybir.dt.float8_e4m3fn_x4
FP4X4 = mybir.dt.float4_e2m1fn_x4
COPY = mybir.ActivationFunctionType.Copy
ADD = mybir.AluOpType.add
SUB = mybir.AluOpType.subtract
MAX = mybir.AluOpType.max

P = 128
PACK = 4
D, K, T, U, X, I, O, Q = 512, 512, 1024, 1024, 1024, 512, 2048, 128
BANK = 512
HALF = I // 2
LIST_HALF = HALF // 16
C0_PASS = 256
C0_PASSES = ((0, 256), (256, 512), (512, 768), (768, 1024))
R_POOL = 640
CC_VECTOR = 704

FLOPS = 2 * Q * (D * K + K * T + K * U + D * X)


def tile_attend_jointthree_sidethree_kernel(
    tc, states, wq_words, wq_scales, cache_words, cache_scales, draft_words, draft_scales,
    arch_words, arch_scales, offs, offs2, offs3, offs4, offs5, out,
):
    nc = tc.nc
    with ExitStack() as ctx:
        sb = ctx.enter_context(tc.tile_pool(name="sb", bufs=1))
        ps = ctx.enter_context(tc.psum_pool(name="ps", bufs=1))

        def load_plane_direct(name, scales, width):
            plane = sb.tile([P, width], U8, name=name, align_bytes=64)
            rows = scales[0].bitcast(I32)
            for g in range(4):
                nc.sync.dma_start(out=plane[:].bitcast(I32)[32 * g : 32 * g + 4, :], in_=rows[4 * g : 4 * g + 4, :])
            return plane

        def load_plane(queue, plane, scales):
            rows = scales[0].bitcast(I32).rearrange("(g h f) n -> g f h n", h=2, g=2)
            words = plane[:].bitcast(I32).rearrange("p (h n) -> p h n", h=2)
            for g in range(2):
                queue.dma_start(out=words[64 * g : 64 * g + 4, :, :], in_=rows[g])

        def spread_plane(plane, width):
            words = plane[:].bitcast(I32)
            n = width // 4
            for g in range(2):
                nc.vector.tensor_copy(out=words[64 * g + 32 : 64 * g + 36, 0:n], in_=words[64 * g : 64 * g + 4, n : 2 * n])

        def load_list(name, source):
            tile = sb.tile([P, I // 16], U16, name=name)
            nc.sync.dma_start(tile[:], source)
            return tile

        wq_plane = sb.tile([P, 2 * K], U8, name="wq_plane", align_bytes=64)
        nc.vector.memset(wq_plane[:].bitcast(I32), 0)

        states_raw = sb.tile([P, PACK, Q], F32, name="states_raw")
        nc.sync.dma_start(out=states_raw[:], in_=states.rearrange("(p t) q -> p t q", t=PACK))
        arch_plane = load_plane_direct("arch_plane", arch_scales, X)
        arch_src = arch_words[0].rearrange("p n t -> p (n t)").bitcast(I32)
        arch_w = []
        for h in range(2):
            tile = sb.tile([P, BANK], U32, name="arch_w%d" % h, align_bytes=64)
            nc.sync.dma_start(out=tile[:].bitcast(I32), in_=arch_src[:, h * BANK : (h + 1) * BANK])
            arch_w.append(tile)
        wq_raw = sb.tile([P, K], U32, name="wq_raw", align_bytes=64)
        nc.sync.dma_start(out=wq_raw[:].bitcast(I32), in_=wq_words[0].rearrange("p n t -> p (n t)").bitcast(I32))
        load_plane(nc.sync, wq_plane, wq_scales)
        list1 = load_list("list1", offs)
        list2 = load_list("list2", offs2)
        cache_w = sb.tile([P, T], U32, name="cache_w", align_bytes=64)
        nc.sync.dma_start(out=cache_w[:].bitcast(I32), in_=cache_words[0].rearrange("p n t -> p (n t)").bitcast(I32))
        cache_plane = load_plane_direct("cache_plane", cache_scales, T)
        draft_w = sb.tile([P, 2 * U], U8, name="draft_w", align_bytes=64)
        nc.sync.dma_start(out=draft_w[:].bitcast(I32), in_=draft_words[0].bitcast(I32))
        draft_plane = load_plane_direct("draft_plane", draft_scales, U)
        list3 = load_list("list3", offs3)
        list4 = load_list("list4", offs4)
        list5 = load_list("list5", offs5)

        f1 = sb.tile([P, O], F32, name="f1")
        nc.vector.memset(f1[:], 0.0)

        states_bf = sb.tile([P, Q, PACK], BF16, name="states_bf", tag="states_then_deal", align_bytes=64)
        for h in range(2):
            cols = slice(h * Q // 2, (h + 1) * Q // 2)
            nc.vector.tensor_copy(out=states_bf[:, cols, :], in_=states_raw[:, :, cols].rearrange("p t q -> p q t"))
        states_codes = sb.tile([P, Q], U32, name="states_codes", align_bytes=64)
        states_plane = sb.tile([P, Q], U8, name="states_plane", align_bytes=64)
        for h in range(2):
            cols = slice(h * Q // 2, (h + 1) * Q // 2)
            nc.vector.quantize_mx(
                out=states_codes[:, cols].bitcast(FP8X4), scales=states_plane[:, cols],
                in_=states_bf[:, cols, :].rearrange("p q t -> p (q t)"),
            )
        spread_plane(wq_plane, K)
        wq_dealt_plane = sb.tile([P, K], U8, name="wq_dealt_plane", tag="states_then_deal", align_bytes=64)
        nc.vector.tensor_copy(
            out=wq_dealt_plane[:].rearrange("p (t m) -> p m t", t=PACK),
            in_=wq_plane[:, 0:K].rearrange("p (m t) -> p m t", t=PACK),
        )
        wq_dealt = sb.tile([P, K], U32, name="wq_dealt", align_bytes=64)
        nc.vector.tensor_copy(
            out=wq_dealt[:].bitcast(I32).rearrange("p (t m) -> p m t", t=PACK),
            in_=wq_raw[:].bitcast(I32).rearrange("p (m t) -> p m t", t=PACK),
        )

        c0 = sb.tile([P, X], F32, name="c0")
        c0_ps = []
        for j, (lo, hi) in enumerate(C0_PASSES):
            bank = ps.tile([P, hi - lo], F32, name="c0_ps%d" % j, tag="bank%d" % j)
            nc.tensor.matmul_mx(
                out=bank[:], lhsT=states_codes[:].bitcast(FP8X4), lhsT_scale=states_plane[:],
                rhs=arch_w[lo // BANK][:, lo % BANK : lo % BANK + hi - lo].bitcast(FP8X4),
                rhs_scale=arch_plane[:, lo:hi], start=True, stop=True,
            )
            nc.scalar.copy(out=c0[:, lo:hi], in_=bank[:])
            c0_ps.append(bank)

        qv_ps = ps.tile([P, PACK, Q], F32, name="qv_ps", tag="bank7")
        for t in range(PACK):
            nc.tensor.matmul_mx(
                out=qv_ps[:, t, :], lhsT=wq_dealt[:, t * P : (t + 1) * P].bitcast(FP8X4),
                lhsT_scale=wq_dealt_plane[:, t * P : (t + 1) * P],
                rhs=states_codes[:].bitcast(FP8X4), rhs_scale=states_plane[:], start=True, stop=True,
            )

        def pick_and_place(h, tag):
            picked = sb.tile([P, HALF], F32, name="c0_picked%d" % h, tag=tag, align_bytes=64)
            cols = slice(h * LIST_HALF, (h + 1) * LIST_HALF)
            if h == 0:
                nc.scalar.activation(picked[:], c0[:].indirect(list1[:, cols]), COPY)
            else:
                nc.vector.tensor_copy(out=picked[:], in_=c0[:].indirect(list1[:, cols]))
            nc.scalar.activation(f1[:].indirect(list2[:, cols]), picked[:], COPY)

        pick_and_place(0, "picked0")
        qv_bf = sb.tile([P, Q, PACK], BF16, name="qv_bf", tag="qv_then_f2", align_bytes=64)
        nc.vector.tensor_copy(out=qv_bf[:], in_=qv_ps[:].rearrange("p t q -> p q t"))
        qv_codes = sb.tile([P, Q], U32, name="qv_codes", align_bytes=64)
        qv_plane = sb.tile([P, Q], U8, name="qv_plane", align_bytes=64)
        nc.vector.quantize_mx(
            out=qv_codes[:].bitcast(FP8X4), scales=qv_plane[:],
            in_=qv_bf[:].rearrange("p q t -> p (q t)"),
        )

        pick_and_place(1, "picked1")
        f2 = sb.tile([P, X], F32, name="f2", tag="qv_then_f2", align_bytes=64)
        nc.vector.memset(f2[:], 0.0)

        ab_ps = []
        for j in range(O // BANK):
            bank = ps.tile([P, BANK], F32, name="ab_ps%d" % j, tag="bank%d" % (4 + j))
            lo = (j * BANK) % T
            if j * BANK < T:
                words = cache_w[:, lo : lo + BANK].bitcast(FP8X4)
                plane = cache_plane[:, lo : lo + BANK]
            else:
                words = draft_w[:, 2 * lo : 2 * (lo + BANK)].bitcast(FP4X4)
                plane = draft_plane[:, lo : lo + BANK]
            nc.tensor.matmul_mx(
                out=bank[:], lhsT=qv_codes[:].bitcast(FP8X4), lhsT_scale=qv_plane[:],
                rhs=words, rhs_scale=plane, start=True, stop=True,
            )
            ab_ps.append(bank)

        def pieces(lo, hi, width):
            return [(max(lo, b), min(hi, b + width)) for b in range(lo // width * width, hi, width)]

        ab_head = sb.tile([P, R_POOL], F32, name="ab_head")
        for lo, hi in pieces(0, R_POOL, BANK):
            nc.vector.tensor_copy(out=ab_head[:, lo:hi], in_=ab_ps[lo // BANK][:, lo % BANK : lo % BANK + hi - lo])

        r = sb.tile([P, O], F32, name="r")
        nc.gpsimd.tensor_tensor(out=r[:, 0:R_POOL], in0=ab_head[:], in1=f1[:, 0:R_POOL], op=SUB)
        for lo, hi in pieces(R_POOL, O, BANK):
            nc.vector.tensor_tensor(
                out=r[:, lo:hi], in0=ab_ps[lo // BANK][:, lo % BANK : lo % BANK + hi - lo], in1=f1[:, lo:hi], op=SUB
            )

        r_picked = sb.tile([P, I], F32, name="r_picked")
        nc.vector.tensor_copy(out=r_picked[:], in_=r[:].indirect(list3[:]))
        nc.scalar.activation(f2[:].indirect(list4[:]), r_picked[:], COPY)

        cc = sb.tile([P, X], F32, name="cc")
        nc.gpsimd.tensor_tensor(out=cc[:, CC_VECTOR:X], in0=c0[:, CC_VECTOR:X], in1=f2[:, CC_VECTOR:X], op=ADD)
        for lo, hi in pieces(0, CC_VECTOR, C0_PASS):
            nc.vector.tensor_tensor(
                out=cc[:, lo:hi], in0=c0_ps[lo // C0_PASS][:, lo % C0_PASS : lo % C0_PASS + hi - lo],
                in1=f2[:, lo:hi], op=ADD,
            )

        cc_picked = [sb.tile([P, HALF], F32, name="cc_picked%d" % h) for h in range(2)]
        nc.vector.tensor_copy(out=cc_picked[0][:], in_=cc[:].indirect(list5[:, 0:LIST_HALF]))
        nc.scalar.activation(cc_picked[1][:], cc[:].indirect(list5[:, LIST_HALF : 2 * LIST_HALF]), COPY)
        for h, queue in enumerate((nc.sync, nc.scalar)):
            cols = slice(h * HALF, (h + 1) * HALF)
            result = sb.tile([P, HALF], F32, name="result%d" % h)
            nc.vector.tensor_tensor(out=result[:], in0=cc_picked[h][:], in1=r_picked[:, cols], op=MAX)
            queue.dma_start(out=out[:, cols], in_=result[:])
